import numpy as np
CORES = [12,28,60,100,156,228]
N = 6
R, E = 4096, 2048
CAPP = 1024
def entries(a): return a.T.reshape(-1)
def pack(v, P): return np.ascontiguousarray(np.asarray(v, np.int32).reshape(-1, P).T)
def lists(rng, how):
    n = N * E; q = np.arange(n) // E
    P = rng.permutation(np.repeat(np.arange(N * N), CAPP))[:n]
    if how == "full":
        a = rng.integers(0, N); z = np.delete(np.arange(N), a); o = rng.permutation(N * N); o = o[(o // N != a) & (o % N != a) & (o // N != o % N)]
        C = np.concatenate([N * a + rng.permutation(z), [(N + 1) * a], N * rng.permutation(z) + a, o])[:n // CAPP]
        L = np.repeat(C, CAPP).reshape(N, E); s, t = 1 + 2 * rng.integers(0, CAPP // 8, 2); t += 2 * (CAPP // 8)
        L[0, :s], L[1, :s] = C[E // CAPP], C[0]; L[0, s:s + t], L[N - 1, E - t:] = C[-1], C[0]
        L = L[rng.permutation(N)]; L[0] = L[0].reshape(16, -1).T.reshape(-1)
        for r in range(1, N, 2): L[r] = rng.permutation(L[r])
        P = L.reshape(-1)
    if how == "same":
        o = np.arange(N * N); o = rng.permutation(np.repeat(o[o % (N + 1) != 0], CAPP))[:n - N * CAPP].reshape(N, E - CAPP)
        P = np.stack([rng.permutation(np.append(o[r], np.full(CAPP, (N + 1) * r))) for r in range(N)]).reshape(-1)
    if how == "cross":
        d = np.stack([rng.permutation(1 + np.arange(E) % (N - 1)) for r in range(N)]).reshape(-1); a = 1 + rng.integers(0, N - 2, N); a += a >= N - np.arange(N)
        P = (q + a[d]) % N * N + (q + a[d] + d) % N
    if how == "edge": k = rng.permutation(n); P = k % (N * N)
    h, g = P // N, P % N; u, v = rng.integers(0, R, n), rng.integers(0, R, n)
    if how == "alike": u, v = rng.integers(0, R, N * N)[P], rng.integers(0, R, N * N)[P]
    if how == "edge": u, v = (R - 1) * (k // (N * N) % 2), (R - 1) * (k // (2 * N * N) % 2)
    if how == "full": u, v = (np.stack([rng.permutation(R)[np.arange(E) % R] for r in range(N)]).reshape(-1) for _ in range(2))
    if how == "same": v = u
    return {"pi": np.stack([pack(w, 16) for w in (R * h + u).reshape(N, E)]), "pj": np.stack([pack(w, 16) for w in (R * g + v).reshape(N, E)])}
def setup_inputs(rng):
    return dict({"ta": rng.standard_normal((N, 128, R), dtype=np.float32), "tb": rng.standard_normal((N, 128, R), dtype=np.float32)}, **lists(rng, "uniform"))
def setup_inputs_alike(rng):
    d = setup_inputs(rng); d.update(lists(rng, "alike"))
    for k in ("ta", "tb"): d[k] = (d[k].astype(np.float32) * 1024.0).astype(d[k].dtype)
    return d
def setup_inputs_cross(rng):
    d = setup_inputs(rng); d.update(lists(rng, "cross"))
    for k in ("ta", "tb"): d[k] = (d[k].astype(np.float32) * (1 / 1024.0)).astype(d[k].dtype)
    return d
def setup_inputs_edge(rng):
    d = setup_inputs(rng); d.update(lists(rng, "edge"))
    return d
def setup_inputs_full(rng):
    d = setup_inputs(rng); d.update(lists(rng, "full"))
    return d
def setup_inputs_same(rng):
    d = setup_inputs(rng); d.update(lists(rng, "same"))
    return d
def check_inputs(x):
    bad = []
    if x["pi"].min() < 0 or x["pi"].max() >= N * R: bad.append("pi out of range")
    if x["pj"].min() < 0 or x["pj"].max() >= N * R: bad.append("pj out of range")
    if not bad and int(np.bincount((x["pi"] // R * N + x["pj"] // R).reshape(-1), minlength=N * N).max()) > CAPP: bad.append("more than CAPP pairs with i in one rank's part of TA and j in one rank's part of TB")
    return bad
def reference(ta, tb, pi, pj):
    A, B = np.concatenate(list(ta), axis=1).astype(np.float64), np.concatenate(list(tb), axis=1).astype(np.float64)
    y = []
    for r in range(N):
        i, j = entries(pi[r]), entries(pj[r])
        y.append((A[:, i] * B[:, j]).sum(axis=0))
    return {"y": np.stack(y).reshape(N, -1, 16).transpose(0, 2, 1).astype(np.float32)}

from concourse.bass import DstId, RemoteDMATransfer
from concourse.mybir import AluOpType, ActivationFunctionType

N, R, E = 6, 4096, 2048
NC = 6
T96 = 96
HALF = NC * 512
WIN = 2 * HALF
DUMPW = 3072
CH = 1024

f32, bf16, i32, u16 = "float32", "bfloat16", "int32", "uint16"
SCRATCH = {
    "li": ("sbuf", [128, 32], i32), "ci": ("sbuf", [128, 32], i32), "c8": ("sbuf", [128, 32], i32),
    "src": ("sbuf", [128, 64], f32), "own": ("sbuf", [128, 64], f32), "land": ("sbuf", [128, 192], f32),
    "kc": ("sbuf", [128, T96], f32), "msk": ("sbuf", [128, 576], bf16), "cnt": ("sbuf", [128, 576], bf16),
    "rst": ("sbuf", [128, 576], bf16), "cc": ("sbuf", [128, 576], bf16), "avg": ("sbuf", [128, 128], bf16),
    "six": ("sbuf", [128, 128], bf16), "tri": ("sbuf", [128, 128], bf16),
    "diff": ("sbuf", [128, 128], i32), "dif15": ("sbuf", [128, 128], i32), "seld": ("sbuf", [128, 8], i32),
    "dump": ("sbuf", [128, T96], f32), "merge": ("sbuf", [128, 128], f32), "sel": ("sbuf", [128, 8], f32),
    "ident": ("sbuf", [128, 128], f32), "ones": ("sbuf", [128, 128], f32),
    "w1": ("sbuf", [128, T96], f32), "w2": ("sbuf", [128, T96], f32), "w3": ("sbuf", [128, T96], f32),
    "pa": ("sbuf", [128, 288], f32), "s4": ("sbuf", [128, 384], f32), "e2": ("sbuf", [128, 192], f32),
    "f1": ("sbuf", [128, T96], f32), "ft": ("sbuf", [128, T96], f32), "off": ("sbuf", [128, T96], u16),
    "val": ("sbuf", [128, 1536], f32), "win": ("sbuf", [128, WIN + DUMPW], f32), "wt": ("sbuf", [128, 384], f32),
    "off2": ("sbuf", [128, 384], u16),
    "taw": ("sbuf", [128, R], f32), "tbw": ("sbuf", [128, R], f32), "ga": ("sbuf", [128, NC * 512], f32),
    "ar": ("sbuf", [128, WIN], f32), "bg": ("sbuf", [128, WIN], f32), "sw": ("sbuf", [128, WIN + 16], f32),
    "r1": ("sbuf", [128, T96], f32), "r2": ("sbuf", [128, T96], i32), "r3": ("sbuf", [128, T96], i32),
    "r4": ("sbuf", [128, T96], i32), "r5": ("sbuf", [128, T96], f32), "r6": ("sbuf", [128, T96], f32),
    "r7": ("sbuf", [128, T96], f32), "r8": ("sbuf", [128, T96], f32), "r9": ("sbuf", [128, T96], f32),
    "ro": ("sbuf", [128, T96], u16), "gr": ("sbuf", [128, 1536], f32),
    "rt": ("sbuf", [128, T96], f32), "rtl": ("sbuf", [128, T96], f32), "fin": ("sbuf", [128, T96], f32),
    "yt": ("sbuf", [128, 128], f32),
}
for _k in range(8):
    SCRATCH["ps%d" % _k] = ("psum", [128, 512], f32)

SEMAPHORES = ["lia", "lib", "srcd", "lst", "own", "fw", "loc", "rt", "fin", "v", "cst", "iot", "memw", "memv", "kcd", "mka", "mkb", "sca", "scb",
              "ppa", "ppb", "offd", "vald", "scat", "wrp", "mgd", "off2d", "tbl", "rod", "wrd", "rtd", "fmd", "yd", "yo", "swm"]
for _k in range(6):
    SEMAPHORES += ["ls%d" % _k, "gad%d" % _k, "gg%d" % _k]
for _k in range(4):
    SEMAPHORES += ["ld%d" % _k, "ta%d" % _k]
for _k in range(12):
    SEMAPHORES += ["ars%d" % _k, "bgd%d" % _k, "pr%d" % _k, "mm%d" % _k, "cp%d" % _k]


def pop(m):
    return bin(m).count("1")


def team(rc, T, topo):
    own = [c for c in range(256) if topo.host(c) == topo.host(rc) and topo.chip(c) == topo.chip(rc)
           and all(topo.may_write(c, d) for d in T.cores if d != c)]
    a0 = [c for c in own if topo.die(c) == topo.die(rc)][0]
    a1 = [c for c in own if topo.die(c) != topo.die(rc)][0]
    return rc, a0, a1


def list_routes(q, teams, topo):
    b, a0, a1 = teams[q]
    load = {b: 1.5, a0: 4.0, a1: 4.0}
    targets = [(t, k, r) for r in range(N) if r != q for k, t in (("A", teams[r][1]), ("A", teams[r][2]), ("B", teams[r][0]))]
    targets.sort(key=lambda x: topo.may_write(b, x[0]))
    way = {}
    for t, k, r in targets:
        s = min([c for c in (a0, a1, b) if topo.may_write(c, t)], key=lambda c: load[c])
        load[s] += 1.0
        way[t] = (s, k, r)
    return way


def rank_program(g, core, T, topo):
    teams = [team(c, T, topo) for c in T.cores]
    mine = [(r, t.index(core)) for r, t in enumerate(teams) if core in t]
    if not mine:
        return
    rank, place = mine[0]
    is_b, h = place == 0, place - 1
    B, A0, A1 = teams[rank]
    S, V, P, A, Q = T.sem, g.vector, g.tensor, g.scalar, g.sync
    op, COPY = AluOpType, ActivationFunctionType.Copy
    n = {"v": 0, "loc": 0, "cst": 0}

    def did(dst):
        rid, pid = topo.addr(dst, core)
        return DstId(rid=rid, pnc=pid)

    def send(dst, out, in_, rsem, lsem="loc"):
        rid, pid = topo.addr(dst, core)
        m = topo.mask(core, dst)
        g.remote_dma(out, in_, S[rsem], S[lsem], pid, rid, m)
        n[lsem] = n.get(lsem, 0) + pop(m)

    def cast(dsts, out, in_, rsem, lsem="loc"):
        m = topo.mask(core, dsts[0])
        for d in dsts:
            m &= topo.mask(core, d)
        g.remote_dma_fused([RemoteDMATransfer(dst_ids=[did(d) for d in dsts], dma_engine_mask=m, remote_sem=S[rsem],
                                              srcs=[in_], dsts=[out for d in dsts])], local_sem=S[lsem])
        n[lsem] = n.get(lsem, 0) + pop(m)

    def v(ins):
        ins.then_inc(S["v"], 1)
        n["v"] += 1

    def vw():
        V.wait_ge(S["v"], n["v"])

    def c(ins):
        ins.then_inc(S["cst"], 1)
        n["cst"] += 1

    ways = [list_routes(q, teams, topo) for q in range(N)]

    if is_b:
        Q.dma_start(T.li[:, 0:16], T.pi[:]).then_inc(S["lia"], 16)
        A.dma_start(T.li[:, 16:32], T.pj[:]).then_inc(S["lib"], 16)
        Q.dma_start(T.taw[:, 0:CH], T.ta[:, 0:CH]).then_inc(S["ld0"], 16)
        V.wait_ge(S["lia"], 16)
        V.wait_ge(S["lib"], 16)
        v(V.tensor_scalar(out=T.ci[:], in0=T.li[:], scalar1=12, scalar2=None, op0=op.arith_shift_right))
        V.tensor_copy(T.src[:, 0:16], T.li[:, 0:16]).then_inc(S["srcd"], 1)
        V.tensor_copy(T.src[:, 32:48], T.li[:, 16:32]).then_inc(S["srcd"], 1)
        vw()
        v(V.tensor_scalar(out=T.c8[:], in0=T.ci[:], scalar1=8, scalar2=None, op0=op.mult))
        vw()
        V.tensor_tensor(T.src[:, 16:32], T.c8[:, 0:16], T.ci[:, 16:32], op.add).then_inc(S["srcd"], 1)
        V.tensor_tensor(T.src[:, 48:64], T.c8[:, 16:32], T.ci[:, 0:16], op.add).then_inc(S["srcd"], 1)

    g.iota(T.diff[:], [[-1, 128]], 128, 1).then_inc(S["iot"], 1)
    g.iota(T.seld[:], [[-16, 2], [-32, 4]], 0, 1).then_inc(S["iot"], 1)
    g.iota(T.dump[:], [[512, 3], [0, 2], [1, 16]], WIN, 16, allow_small_or_imprecise_dtypes=True).then_inc(S["iot"], 1)
    lo, hi = (0, WIN) if is_b else (h * HALF, (h + 1) * HALF)
    c(V.memset(T.rst[:], 1.0))
    V.memset(T.val[:], 0.0).then_inc(S["memv"], 1)
    for k in range(NC):
        c(V.memset(T.cc[:, k * T96:(k + 1) * T96], float(k)))
    c(V.memset(T.avg[:], 1.0 / 128))
    c(V.memset(T.six[:], 6.0))
    V.wait_ge(S["cst"], n["cst"])
    for k in range(NC):
        c(V.memset(T.rst[:, k * T96:k * T96 + 1], 0.0))
    V.wait_ge(S["iot"], 3)
    c(V.tensor_scalar(out=T.tri[:], in0=T.diff[:], scalar1=128.0, scalar2=-6.0, op0=op.is_ge, op1=op.mult))
    v(V.tensor_scalar(out=T.dif15[:], in0=T.diff[:], scalar1=15, scalar2=None, op0=op.bitwise_and))
    vw()
    c(V.tensor_scalar(out=T.merge[:], in0=T.dif15[:], scalar1=0.0, scalar2=None, op0=op.is_equal))
    if is_b:
        c(V.memset(T.ones[:], 1.0))
        c(V.memset(T.sw[:, WIN:WIN + 16], 0.0))
        c(V.tensor_scalar(out=T.sel[:], in0=T.seld[:], scalar1=0.0, scalar2=None, op0=op.is_equal))
        c(V.tensor_scalar(out=T.ident[:], in0=T.diff[:], scalar1=128.0, scalar2=None, op0=op.is_equal))
    V.memset(T.win[:, lo:hi], 0.0).then_inc(S["memw"], 1)

    def relay():
        a = [t for t, w in ways[rank].items() if w[0] == core and w[1] == "A"]
        b = [t for t, w in ways[rank].items() if w[0] == core and w[1] == "B"]
        src = T.src if is_b else T.own
        for who, x in ((a, 0), (b, 32)):
            if who:
                cast(who, T.land[:, rank * 32:(rank + 1) * 32], src[:, x:x + 32], "ls%d" % rank)

    if is_b:
        g.wait_ge(S["srcd"], 4)
        cast([A0, A1], T.own[:], T.src[:], "own", "lst")
        relay()
        A.wait_ge(S["lst"], n["lst"])
        A.dma_start(T.taw[:, CH:2 * CH], T.ta[:, CH:2 * CH]).then_inc(S["ld1"], 16)
        Q.wait_ge(S["lst"], n["lst"])
        Q.dma_start(T.taw[:, 2 * CH:3 * CH], T.ta[:, 2 * CH:3 * CH]).then_inc(S["ld2"], 16)
        A.dma_start(T.taw[:, 3 * CH:], T.ta[:, 3 * CH:]).then_inc(S["ld3"], 16)
        for k in range(4):
            g.wait_ge(S["ld%d" % k], 16)
            send((A0, A1)[k % 2], T.taw[:, k * CH:(k + 1) * CH], T.taw[:, k * CH:(k + 1) * CH], "ta%d" % k, "fw")
        A.wait_ge(S["fw"], n["fw"])
        for k in range(4):
            A.dma_start(T.tbw[:, k * CH:(k + 1) * CH], T.tb[:, k * CH:(k + 1) * CH]).then_inc(S["tbl"], 16)
    else:
        g.wait_ge(S["own"], pop(topo.mask(B, core)))
        relay()
        for k in (h, h + 2):
            g.wait_ge(S["ta%d" % k], pop(topo.mask(B, core)))
            send((A1, A0)[h], T.taw[:, k * CH:(k + 1) * CH], T.taw[:, k * CH:(k + 1) * CH], "ta%d" % k)

    own, ox, osem, ocnt = (T.src, 32, "srcd", 4) if is_b else (T.own, 0, "own", pop(topo.mask(B, core)))
    order = [rank] + [q for q in range(N) if q != rank]
    Q.wait_ge(S["memv"], 1)
    for q in order:
        if q == rank:
            buf, x, sm, ct = own, ox, osem, ocnt
        else:
            buf, x, sm, ct = T.land, q * 32, "ls%d" % q, pop(topo.mask(ways[q][core][0], core))
        V.wait_ge(S[sm], ct)
        V.tensor_copy(T.kc[:, q * 16:(q + 1) * 16], buf[:, x + 16:x + 32]).then_inc(S["kcd"], 1)
        Q.wait_ge(S[sm], ct)
        Q.dma_start(T.val[16 * (q % 2)::32, (q // 2) * 512:(q // 2 + 1) * 512], buf[:, x:x + 16]).then_inc(S["vald"], 16)
    V.wait_ge(S["cst"], n["cst"])
    V.wait_ge(S["kcd"], 6)
    for k in range(NC):
        V.tensor_scalar(out=T.msk[:, k * T96:(k + 1) * T96], in0=T.kc[:], scalar1=float(8 * rank + k), scalar2=None,
                        op0=op.is_equal).then_inc(S["mka" if k < 3 else "mkb"], 1)
    for k in range(2):
        V.wait_ge(S[("mka", "mkb")[k]], 3)
        sl = slice(k * 288, (k + 1) * 288)
        V.tensor_tensor_scan(T.cnt[:, sl], T.rst[:, sl], T.msk[:, sl], 0.0, op.mult, op.add).then_inc(S[("sca", "scb")[k]], 1)
    P.wait_ge(S["cst"], n["cst"])
    for k in range(2):
        P.matmul([T.ps0, T.ps1][k][:, 0:288], T.avg[:], T.cc[:, k * 288:(k + 1) * 288], True, False)
    for k in range(2):
        P.wait_ge(S[("mka", "mkb")[k]], 3)
        P.matmul([T.ps0, T.ps1][k][:, 0:288], T.tri[:], T.msk[:, k * 288:(k + 1) * 288], False, False)
    for k in range(2):
        P.wait_ge(S[("sca", "scb")[k]], 1)
        P.matmul([T.ps0, T.ps1][k][:, 0:288], T.six[:], T.cnt[:, k * 288:(k + 1) * 288], False, True).then_inc(S[("ppa", "ppb")[k]], 1)
    v(V.tensor_scalar(out=T.w1[:], in0=T.kc[:], scalar1=float(8 * rank), scalar2=None, op0=op.is_lt))
    v(V.tensor_scalar(out=T.w2[:], in0=T.kc[:], scalar1=float(8 * rank + 5), scalar2=None, op0=op.is_gt))
    vw()
    v(V.tensor_tensor(T.w3[:], T.w1[:], T.w2[:], op.add))
    vw()
    v(V.tensor_tensor(T.s4[:, 288:384], T.w3[:], T.dump[:], op.mult))
    V.wait_ge(S["sca"], 1)
    V.wait_ge(S["scb"], 1)
    V.wait_ge(S["ppa"], 1)
    v(V.tensor_tensor(T.pa[:], T.ps0[:, 0:288], T.msk[:, 0:288], op.mult))
    V.wait_ge(S["ppb"], 1)
    v(V.tensor_tensor(T.ps2[:, 0:288], T.ps1[:, 0:288], T.msk[:, 288:576], op.mult))
    vw()
    v(V.tensor_tensor(T.s4[:, 0:288], T.ps2[:, 0:288], T.pa[:], op.add))
    vw()
    v(V.tensor_tensor(T.e2[:], T.s4[:, 0:192], T.s4[:, 192:384], op.add))
    vw()
    v(V.tensor_tensor(T.f1[:], T.e2[:, 0:96], T.e2[:, 96:192], op.add))
    vw()
    v(V.transpose(T.ft[:], T.f1[:]))
    vw()
    v(V.tensor_copy(T.off[:], T.ft[:]))
    vw()
    V.wait_ge(S["vald"], 96)
    V.wait_ge(S["memw"], 1)
    V.wait_ge(S["memv"], 1)
    V.tensor_copy(T.win[:, 0:WIN + DUMPW].indirect(T.off[:, 0:T96]), T.val[:, 0:1536]).then_inc(S["scat"], 1)
    halves = (0, 1) if is_b else (h,)
    Q.wait_ge(S["memw"], 1)
    Q.wait_ge(S["scat"], 1)
    for k, hh in enumerate(halves):
        Q.dma_start(T.wt[:, k * 192:(k + 1) * 192], T.win[0:128:16, hh * HALF:(hh + 1) * HALF]).then_inc(S["wrp"], 16)
    nh = len(halves)
    P.wait_ge(S["wrp"], 16 * nh)
    for x in range(NC):
        for k in range(nh):
            m = P.matmul(T.ps3[:, (x * nh + k) * 32:(x * nh + k + 1) * 32], T.merge[:], T.wt[:, k * 192 + x:(k + 1) * 192:6], True, True)
    m.then_inc(S["mgd"], 1)
    V.wait_ge(S["mgd"], 1)
    V.wait_ge(S["scat"], 1)
    w = 192 * nh
    V.tensor_scalar(out=T.off2[:, 0:w], in0=T.ps3[:, 0:w], scalar1=float(-R * rank), scalar2=0.0, op0=op.add, op1=op.max).then_inc(S["off2d"], 1)
    V.wait_ge(S["off2d"], 1)
    A.wait_ge(S["off2d"], 1)

    cross = [[q for q in range(N) if q != r and not topo.may_write(teams[r][0], teams[q][0])] for r in range(N)]
    if not is_b:
        for k in range(4):
            cnt = pop(topo.mask(B if k % 2 == h else (A1, A0)[h], core))
            V.wait_ge(S["ta%d" % k], cnt)
            A.wait_ge(S["ta%d" % k], cnt)
        g.wait_ge(S["ta%d" % (1 - h)], pop(topo.mask((A1, A0)[h], core)))
        g.wait_ge(S["ta%d" % (3 - h)], pop(topo.mask((A1, A0)[h], core)))
        dests = [(rank + k) % N for k in range(1, N)] + [rank]
        for k, d in enumerate(dests):
            src = T.taw[:, 0:R].indirect(T.off2[:, d * 32:(d + 1) * 32])
            out = T.ga[:, d * 512:(d + 1) * 512]
            if k % 2 == 0:
                V.tensor_copy(out, src).then_inc(S["gad%d" % d], 1)
            else:
                A.activation(out, src, COPY).then_inc(S["gad%d" % d], 1)
            g.wait_ge(S["gad%d" % d], 1)
            ch = rank * 2 + h
            send(teams[d][0], T.ar[:, ch * 512:(ch + 1) * 512], out, "ars%d" % ch)
        g.wait_ge(S["rt"], pop(topo.mask(B, core)))
        for q in cross[rank][h::2]:
            send(teams[q][0], T.fin[:, rank * 16:(rank + 1) * 16], T.rtl[:, q * 16:(q + 1) * 16], "fin")
        g.wait_ge(S["loc"], n["loc"])
        return

    seq = [2 * ((rank - k) % N) + hh for k in list(range(1, N)) + [0] for hh in (0, 1)]
    V.wait_ge(S["tbl"], 64)
    A.wait_ge(S["tbl"], 64)
    for k, ch in enumerate(seq):
        src = T.tbw[:, 0:R].indirect(T.off2[:, ch * 32:(ch + 1) * 32])
        out = T.bg[:, ch * 512:(ch + 1) * 512]
        (V.tensor_copy(out, src) if k % 2 == 0 else A.activation(out, src, COPY)).then_inc(S["bgd%d" % ch], 1)
    v(V.tensor_scalar(out=T.r1[:], in0=T.ft[:], scalar1=1.0 / 6, scalar2=-5.0 / 12, op0=op.mult, op1=op.add))
    v(V.tensor_scalar(out=T.r5[:], in0=T.ft[:], scalar1=float(WIN), scalar2=8192.0, op0=op.is_ge, op1=op.mult))
    v(V.tensor_scalar(out=T.r6[:], in0=T.ft[:], scalar1=1024.0, scalar2=None, op0=op.mult))
    vw()
    v(V.tensor_copy(T.r2[:], T.r1[:]))
    v(V.tensor_tensor(T.r7[:], T.r5[:], T.r6[:], op.add))
    vw()
    v(V.tensor_scalar(out=T.r3[:], in0=T.r2[:], scalar1=5, scalar2=None, op0=op.arith_shift_right))
    v(V.tensor_scalar(out=T.r4[:], in0=T.r2[:], scalar1=9, scalar2=None, op0=op.arith_shift_right))
    v(V.tensor_scalar(out=T.r5[:], in0=T.r2[:], scalar1=-6128.0, scalar2=None, op0=op.mult))
    vw()
    v(V.tensor_scalar(out=T.r6[:], in0=T.r3[:], scalar1=-511.0, scalar2=None, op0=op.mult))
    v(V.tensor_scalar(out=T.r8[:], in0=T.r4[:], scalar1=496.0, scalar2=None, op0=op.mult))
    v(V.tensor_tensor(T.r9[:], T.r7[:], T.r5[:], op.add))
    vw()
    v(V.tensor_tensor(T.r7[:], T.r6[:], T.r8[:], op.add))
    vw()
    v(V.tensor_tensor(T.r1[:], T.r7[:], T.r9[:], op.add))
    vw()
    V.tensor_scalar(out=T.ro[:], in0=T.r1[:], scalar1=float(WIN), scalar2=0.0, op0=op.min, op1=op.max).then_inc(S["rod"], 1)
    V.wait_ge(S["rod"], 1)
    banks = [T.ps4, T.ps5, T.ps6]
    for k, ch in enumerate(seq):
        sl = slice(ch * 512, (ch + 1) * 512)
        V.wait_ge(S["bgd%d" % ch], 1)
        V.wait_ge(S["ars%d" % ch], pop(topo.mask(teams[ch // 2][1 + ch % 2], core)))
        V.tensor_tensor(T.ar[:, sl], T.bg[:, sl], T.ar[:, sl], op.mult).then_inc(S["pr%d" % ch], 1)
        if k >= 3:
            P.wait_ge(S["cp%d" % seq[k - 3]], 1)
        P.wait_ge(S["pr%d" % ch], 1)
        P.matmul(banks[k % 3][:, 0:512], T.ones[:], T.ar[:, sl], True, True).then_inc(S["mm%d" % ch], 1)
        A.wait_ge(S["mm%d" % ch], 1)
        A.activation(T.sw[:, sl], banks[k % 3][:, 0:512], COPY).then_inc(S["cp%d" % ch], 1)

    for ch in range(12):
        V.wait_ge(S["cp%d" % ch], 1)
        A.wait_ge(S["cp%d" % ch], 1)
    A.wait_ge(S["rod"], 1)
    A.wait_ge(S["cst"], n["cst"])
    for k in range(6):
        src = T.sw[:, 0:WIN + 16].indirect(T.ro[:, k * 16:(k + 1) * 16])
        out = T.gr[:, k * 256:(k + 1) * 256]
        (V.tensor_copy(out, src) if k % 2 == 0 else A.activation(out, src, COPY)).then_inc(S["gg%d" % k], 1)
        P.wait_ge(S["gg%d" % k], 1)
        for blk in (2 * k, 2 * k + 1):
            q2, xh = blk // 4, blk % 4
            m = P.matmul(T.ps7[:, q2 * 32 + xh:q2 * 32 + 32:4], T.gr[:, blk * 128:(blk + 1) * 128], T.sel[:], True, True)
    m.then_inc(S["wrd"], 1)
    V.wait_ge(S["wrd"], 1)
    V.tensor_copy(T.rt[:], T.ps7[:, 0:T96]).then_inc(S["rtd"], 1)
    g.wait_ge(S["rtd"], 1)
    cast([A0, A1], T.rtl[:], T.rt[:], "rt")
    for k in range(1, N):
        q = (rank + k) % N
        if q not in cross[rank]:
            send(teams[q][0], T.fin[:, rank * 16:(rank + 1) * 16], T.rt[:, q * 16:(q + 1) * 16], "fin")
    need = sum(pop(topo.mask(teams[q][1 + cross[q].index(rank) % 2] if rank in cross[q] else teams[q][0], core)) for q in range(N) if q != rank)
    P.wait_ge(S["rtd"], 1)
    P.matmul(T.ps0[0:16, 0:128], T.rt[:, rank * 16:(rank + 1) * 16], T.ident[:], True, False)
    P.wait_ge(S["fin"], need)
    rest = [q for q in range(N) if q != rank]
    for q in rest:
        m = P.matmul(T.ps0[0:16, 0:128], T.fin[:, q * 16:(q + 1) * 16], T.ident[:], False, q == rest[-1])
    m.then_inc(S["fmd"], 1)
    V.wait_ge(S["fmd"], 1)
    V.tensor_copy(T.yt[0:16, :], T.ps0[0:16, 0:128]).then_inc(S["yd"], 1)
    Q.wait_ge(S["yd"], 1)
    Q.dma_start(T.y[:], T.yt[0:16, :]).then_inc(S["yo"], 16)
    Q.wait_ge(S["yo"], 16)
    g.wait_ge(S["loc"], n["loc"])
